import numpy as np
import ml_dtypes


def mxq(x, axis, fmt="e4m3"):
    dtype, down = {"e4m3": (ml_dtypes.float8_e4m3fn, 7), "e5m2": (ml_dtypes.float8_e5m2, 14)}[fmt]
    v = np.moveaxis(np.asarray(x, np.float32).astype(ml_dtypes.bfloat16).astype(np.float64), axis, -1)
    blocks = v.reshape(v.shape[:-1] + (-1, 32))
    amax = np.abs(blocks).max(-1, keepdims=True)
    byte = np.maximum(np.where(amax > 0, np.frexp(amax)[1] - 1 + 127, 0) - down, 1)
    scale = np.exp2(byte - 127.0)
    codes = (blocks / scale).astype(np.float32).astype(dtype).astype(np.float64)
    return np.moveaxis((codes * scale).reshape(v.shape), -1, axis)


WIDE = False


def mx_kscale(k):
    if not WIDE:
        return np.ones(k)
    levels = np.array([10, -10, 5, -5, 0])
    if k % 512:
        return np.exp2(np.random.permutation(np.resize(levels, k // 32))).repeat(32)
    a = np.empty((k // 512, 16))
    for p in range(k // 512):
        a[p, :8] = np.random.permutation(np.resize(levels, 8))
        for g in range(8):
            far = levels[np.abs(levels - a[p, g]) >= 10]
            a[p, g + 8] = far[np.random.randint(len(far))]
    return np.exp2(a.ravel()).repeat(32)


def f64(x):
    return np.asarray(x).astype(np.float64)


def striped(idx):
    return np.tile(idx.reshape(-1, 16).T, (8, 1)).astype(np.uint16)


def unstriped(offs):
    return offs[:16].T.reshape(-1).astype(np.int64)


def pack_weight(w):
    k, n = w.shape
    w = f64(np.asarray(w, np.float32).astype(ml_dtypes.bfloat16)).reshape(k // 32, 32, n)
    amax = np.abs(w).max(1)
    byte = np.clip(np.where(amax > 0, np.frexp(amax)[1] - 1 + 127 - 7, 1), 1, 254)
    scaled = (w * np.exp2(127.0 - byte)[:, None, :]).reshape(k, n).astype(np.float32)
    words = np.ascontiguousarray(scaled.reshape(k // 512, 128, 4, n).transpose(0, 1, 3, 2)).astype(ml_dtypes.float8_e4m3fn).view(np.uint8)
    return words, np.ascontiguousarray(byte.astype(np.uint8).reshape(k // 512, 16, n))


def unpack_weight(words, scales):
    g, p, n, _ = words.shape
    vals = np.ascontiguousarray(words).view(ml_dtypes.float8_e4m3fn).astype(np.float64) * np.repeat(np.exp2(scales.astype(np.float64) - 127.0), 8, axis=1)[..., None]
    return vals.transpose(0, 1, 3, 2).reshape(g * 512, n)


def relu(v):
    return np.maximum(v, 0.0)


K, T, S, V, W, U = 512, 1024, 512, 256, 2048, 1024
P = 2 ** 7


def setup_inputs():
    n = np.random.standard_normal
    s = mx_kscale(K)[:, None]
    packed_xT = pack_weight(n((K, T)) * s)
    packed_eT = pack_weight(n((K, W)) * s)
    return {
        "x_words": packed_xT[0],
        "x_scales": packed_xT[1],
        "e_words": packed_eT[0],
        "e_scales": packed_eT[1],
        "wq": (n((K, V)) / np.sqrt(K) / s).astype(np.float32),
        "wt": (n((K, V)) / np.sqrt(K) / s).astype(np.float32),
        "disc": (np.random.uniform(0.7, 1.0, (S, 1))).astype(np.float32),
        "rew": (n((S, 1))).astype(np.float32),
        "tau": (np.tile(np.random.uniform(0.05, 0.95, U), (P, 1))).astype(np.float32),
        "ku": (np.tile(np.random.uniform(0.8, 1.2, U), (P, 1))).astype(np.float32),
        "kd": (np.tile(np.random.uniform(0.8, 1.2, U), (P, 1))).astype(np.float32),
        "offs": striped(np.random.permutation(T)[:S]),
        "nxt": striped(np.random.permutation(W)[:S]),
        "pa": striped(np.random.permutation(np.concatenate([np.arange(V), np.random.randint(0, V, U - V)]))),
        "pb": striped(np.random.permutation(np.concatenate([np.arange(V), np.random.randint(0, V, U - V)]))),
    }


def reference(x_words, x_scales, e_words, e_scales, wq, wt, disc, rew, tau, ku, kd, offs, nxt, pa, pb):
    e_nxt = unpack_weight(e_words, e_scales)[:, unstriped(nxt)]
    wtq = mxq(f64(wt), 0, "e4m3")
    h = f64(disc) * (e_nxt.T @ wtq) + f64(rew)
    xq = unpack_weight(x_words, x_scales)[:, unstriped(offs)]
    wqq = mxq(f64(wq), 0, "e4m3")
    y = xq.T @ wqq
    td = h[:, unstriped(pb)] - y[:, unstriped(pa)]
    up = relu(td)
    cu = np.minimum(up, f64(ku)[:1])
    dn = relu(-1.0 * td)
    cd = np.minimum(dn, f64(kd)[:1])
    return f64(tau)[:1] * cu - cd + f64(tau)[:1] * cd

@@ -1,0 +1,233 @@
+from contextlib import ExitStack
+
+import concourse.mybir as mybir
+from concourse.masks import make_identity
+
+K, T, S, V, W, U = 512, 1024, 512, 256, 2048, 1024
+FLOPS = 2 * 2 * K * S * V
+
+F32 = mybir.dt.float32
+BF16 = mybir.dt.bfloat16
+I32 = mybir.dt.int32
+U32 = mybir.dt.uint32
+U16 = mybir.dt.uint16
+U8 = mybir.dt.uint8
+FP8X4 = mybir.dt.float8_e4m3fn_x4
+ALU = mybir.AluOpType
+ACT = mybir.ActivationFunctionType
+
+P = 128
+TB = S // P
+RB = U // P
+CHUNKS = (128, 256, 256, 128, 128, 128)
+SPARE = 96
+VECTOR_FROM = 7
+BANKS = 4
+
+
+def tile_picked_yqrdqn_grad_p_kernel(
+    tc, x_words, x_scales, e_words, e_scales, wq, wt, disc, rew, tau, ku, kd, offs, nxt, pa, pb, out
+):
+    nc = tc.nc
+    with ExitStack() as ctx:
+        keep = ctx.enter_context(tc.tile_pool(name="keep", bufs=1))
+        ring = ctx.enter_context(tc.tile_pool(name="ring", bufs=4))
+        work = ctx.enter_context(tc.tile_pool(name="work", bufs=2))
+        psum = ctx.enter_context(tc.psum_pool(name="psum", bufs=1))
+
+        offs_t = keep.tile([P, S // 16], U16, name="offs_t")
+        nxt_t = keep.tile([P, S // 16], U16, name="nxt_t")
+        pa_t = keep.tile([P, U // 16], U16, name="pa_t")
+        pb_t = keep.tile([P, U // 16], U16, name="pb_t")
+        xw = keep.tile([P, T], I32, name="xw")
+        ew = keep.tile([P, W], I32, name="ew")
+        xs = keep.tile([P, T], U8, name="xs")
+        es = keep.tile([P, W], U8, name="es")
+        wq_raw = keep.tile([P, 4, V], F32, name="wq_raw")
+        wt_raw = keep.tile([P, 4, V], F32, name="wt_raw")
+        rows = keep.tile([P, P], F32, name="rows")
+        ident = keep.tile([P, P], F32, name="ident")
+        y_neg = keep.tile([P, TB * V + SPARE], F32, name="y_neg")
+        h_all = keep.tile([P, TB * V + SPARE], F32, name="h_all")
+
+        nc.gpsimd.memset(xs[:].bitcast(I32), 0)
+        nc.gpsimd.memset(es[:].bitcast(I32), 0)
+        nc.gpsimd.memset(rows[:], 0.0)
+        make_identity(nc, ident[:])
+        nc.gpsimd.memset(y_neg[:, TB * V :], 0.0)
+        nc.gpsimd.memset(h_all[:, TB * V :], 0.0)
+
+        def load_scale_rows(tile, scales):
+            for q in range(4):
+                nc.sync.dma_start(
+                    out=tile[32 * q : 32 * q + 4, :].bitcast(I32),
+                    in_=scales[0, 4 * q : 4 * q + 4, :].bitcast(I32),
+                )
+
+        nc.sync.dma_start(offs_t[:], offs)
+        nc.sync.dma_start(out=xw[:], in_=x_words[0].rearrange("p n t -> p (n t)").bitcast(I32))
+        nc.sync.dma_start(nxt_t[:], nxt)
+        load_scale_rows(xs, x_scales)
+        nc.sync.dma_start(out=wq_raw[:], in_=wq.rearrange("(p j) v -> p j v", j=4))
+        nc.sync.dma_start(out=wt_raw[:], in_=wt.rearrange("(p j) v -> p j v", j=4))
+        load_scale_rows(es, e_scales)
+        nc.sync.dma_start(pa_t[:], pa)
+        nc.sync.dma_start(out=ew[:], in_=e_words[0].rearrange("p n t -> p (n t)").bitcast(I32))
+        nc.sync.dma_start(pb_t[:], pb)
+        nc.sync.dma_start(out=rows[24:28, :], in_=disc.rearrange("(b c) o -> b (c o)", c=P))
+        nc.sync.dma_start(out=rows[28:32, :], in_=rew.rearrange("(b c) o -> b (c o)", c=P))
+        for i, row in enumerate((tau, ku, kd)):
+            nc.sync.dma_start(
+                out=rows[RB * i : RB * (i + 1), :],
+                in_=row[0:1, :].rearrange("o (j c) -> (o j) c", c=P),
+            )
+
+        def gather_words(words, index, name, pieces):
+            codes = keep.tile([P, S], U32, name=name + "_codes", align_bytes=64)
+            n = S // pieces
+            for i in range(pieces):
+                nc.vector.tensor_copy(
+                    codes[:, i * n : (i + 1) * n],
+                    words[:].bitcast(U32).indirect(index[:, i * n // 16 : (i + 1) * n // 16]),
+                )
+            return codes
+
+        def gather_scales(scales, index, name):
+            plane = keep.tile([P, S], U8, name=name + "_plane", align_bytes=64)
+            nc.vector.tensor_copy(plane[:], scales[:].indirect(index[:]))
+            return plane
+
+        def quantize_weight(raw, name):
+            grouped = keep.tile([P, V * 4], BF16, name=name + "_grouped", align_bytes=64)
+            codes = keep.tile([P, V], U32, name=name + "_codes", align_bytes=64)
+            plane = keep.tile([P, V], U8, name=name + "_plane", align_bytes=64)
+            nc.scalar.copy(
+                out=grouped[:].rearrange("p (c i j) -> p c j i", i=4, j=4),
+                in_=raw[:].rearrange("p j (c i) -> p c j i", i=4),
+            )
+            nc.vector.quantize_mx(out=codes[:].bitcast(FP8X4), scales=plane[:], in_=grouped[:])
+            return codes, plane
+
+        def product(picked, weight, b, name):
+            acc = psum.tile([P, 512], F32, name=name, tag="acc", bufs=3)
+            cols = slice(b * P, (b + 1) * P)
+            nc.tensor.matmul_mx(
+                out=acc[:, :V],
+                lhsT=picked[0][:, cols].bitcast(FP8X4),
+                lhsT_scale=picked[1][:, cols],
+                rhs=weight[0][:].bitcast(FP8X4),
+                rhs_scale=weight[1][:],
+                start=True,
+                stop=True,
+            )
+            return acc[:, :V]
+
+        def place(b):
+            return (TB - 1 - b) * V
+
+        x_picked = (gather_words(xw, offs_t, "x", 1), gather_scales(xs, offs_t, "x"))
+        wq_mx = quantize_weight(wq_raw, "wq")
+        e_plane = gather_scales(es, nxt_t, "e")
+        wt_mx = quantize_weight(wt_raw, "wt")
+        for b in range(TB):
+            acc = product(x_picked, wq_mx, b, "y_acc")
+            nc.scalar.activation(y_neg[:, place(b) : place(b) + V], acc, ACT.Copy, scale=-1.0)
+
+        e_picked = (gather_words(ew, nxt_t, "e", 2), e_plane)
+
+        turned = psum.tile([P, 512], F32, name="turned")
+        nc.tensor.transpose(turned[:, :P], rows[:], ident[:])
+        per_t = keep.tile([P, 2 * TB], F32, name="per_t")
+        nc.scalar.copy(per_t[:], turned[:, 24:32])
+        weight = keep.tile([P, 2 * RB], F32, name="weight")
+        slope_dn = keep.tile([P, RB], F32, name="slope_dn")
+        k_pos = keep.tile([P, 2 * RB], F32, name="k_pos")
+        k_neg = keep.tile([P, 2 * RB], F32, name="k_neg")
+        nc.scalar.copy(weight[:, :RB], turned[:, :RB])
+        nc.scalar.activation(weight[:, RB:], turned[:, :RB], ACT.Copy, scale=1.0, bias=-1.0)
+        nc.scalar.activation(slope_dn[:], turned[:, :RB], ACT.Copy, scale=-1.0, bias=1.0)
+        nc.scalar.activation(k_pos[:], turned[:, RB : 3 * RB], ACT.Relu)
+        nc.scalar.activation(k_neg[:], turned[:, RB : 3 * RB], ACT.Relu, scale=-1.0)
+
+        for b in range(TB):
+            acc = product(e_picked, wt_mx, b, "h_acc")
+            nc.scalar.activation(
+                h_all[:, place(b) : place(b) + V],
+                acc,
+                ACT.Identity,
+                scale=per_t[:, b : b + 1],
+                bias=per_t[:, TB + b : TB + b + 1],
+            )
+
+        span = keep.tile([P, 2 * RB], F32, name="span")
+        shift = keep.tile([P, 2 * RB], F32, name="shift")
+        span_lo = keep.tile([P, 2 * RB], F32, name="span_lo")
+        span_hi = keep.tile([P, 2 * RB], F32, name="span_hi")
+        lo = keep.tile([P, 2 * RB], F32, name="lo")
+        hi = keep.tile([P, 2 * RB], F32, name="hi")
+        nc.gpsimd.tensor_tensor(span[:], weight[:], k_pos[:], ALU.mult)
+        nc.gpsimd.tensor_tensor(shift[:], weight[:], k_neg[:], ALU.mult)
+        nc.gpsimd.tensor_scalar(span_lo[:], span[:], 0.0, None, ALU.min)
+        nc.gpsimd.tensor_scalar(span_hi[:], span[:], 0.0, None, ALU.max)
+        nc.gpsimd.tensor_tensor(lo[:], span_lo[:], shift[:], ALU.subtract)
+        nc.gpsimd.tensor_tensor(hi[:], span_hi[:], shift[:], ALU.subtract)
+
+        out_view = out.rearrange("(b p) r -> p b r", p=P)
+
+        def gather_values(table, index, b, r0, width, name):
+            got = ring.tile([P, width], F32, name=name)
+            window = V if width < V else V + SPARE
+            nc.vector.tensor_copy(
+                got[:], table[:, place(b) : place(b) + window].indirect(index[:, r0 // 16 : (r0 + width) // 16])
+            )
+            return got
+
+        def turn(dst, src, start, stop):
+            nc.tensor.matmul(dst, lhsT=src, rhs=ident[:], is_transpose=True, start=start, stop=stop)
+
+        def clip_terms(td, j, n):
+            terms = []
+            clamp = nc.vector if j >= VECTOR_FROM else nc.gpsimd
+            for side, slope in enumerate((weight[:, j : j + 1], slope_dn[:, j : j + 1])):
+                scaled = work.tile([P, n], F32, name="scaled%d" % side)
+                term = work.tile([P, n], F32, name="term%d" % side, bufs=3)
+                c = side * RB + j
+                nc.scalar.activation(scaled[:], td, ACT.Copy, scale=slope)
+                clamp.tensor_scalar(term[:], scaled[:], hi[:, c : c + 1], lo[:, c : c + 1], ALU.min, ALU.max)
+                terms.append(term)
+            return terms
+
+        def finish(terms, bank, j, b0, nb):
+            res = psum.tile([P, nb, P], F32, name="res", tag=bank)
+            for side in range(2):
+                for b in range(nb):
+                    turn(res[:, b, :], terms[side][:, b * P : (b + 1) * P], side == 0 and b == 0, side == 1 and b == nb - 1)
+            staged = work.tile([P, nb, P], F32, name="staged", bufs=4)
+            nc.scalar.copy(staged[:], res[:])
+            nc.sync.dma_start(out=out_view[:, b0 : b0 + nb, j * P : (j + 1) * P], in_=staged[:])
+
+        pending = None
+        unit = 0
+        r0 = 0
+        for width in CHUNKS:
+            blocks = width // P
+            nb = TB // 2 if r0 + width == U else TB
+            y_got = [gather_values(y_neg, pa_t, b, r0, width, "y_got") for b in range(TB)]
+            for b0 in range(0, TB, nb):
+                banks = ["bank%d" % ((unit + i) % BANKS) for i in range(blocks)]
+                unit = unit + blocks
+                tds = [psum.tile([P, nb * P], F32, name="td", tag=bank) for bank in banks]
+                for b in range(nb):
+                    h_got = gather_values(h_all, pb_t, b0 + b, r0, width, "h_got")
+                    for i in range(blocks):
+                        cols = slice(i * P, (i + 1) * P)
+                        turn(tds[i][:, b * P : (b + 1) * P], y_got[b0 + b][:, cols], True, False)
+                        turn(tds[i][:, b * P : (b + 1) * P], h_got[:, cols], False, True)
+                for i in range(blocks):
+                    j = r0 // P + i
+                    terms = clip_terms(tds[i][:], j, nb * P)
+                    if pending is not None:
+                        finish(*pending)
+                    pending = (terms, banks[i], j, b0, nb)
+            r0 = r0 + width
+        finish(*pending)

@@ -17,12 +17,19 @@ ALU = mybir.AluOpType
 ACT = mybir.ActivationFunctionType
 
 P = 128
-TB = S // P
-RB = U // P
-CHUNKS = (128, 256, 256, 128, 128, 128)
+PACK = 4
+LIST_ROWS = 16
+T_BLOCKS = S // P
+R_BLOCKS = U // P
+
+CHUNKS = (256, 256, 256, 128, 128)
+WIDEST = max(CHUNKS)
 SPARE = 96
-VECTOR_FROM = 7
-BANKS = 4
+TD_BANKS = 3
+OUT_BANKS = 3
+SCALED_BUFS = 3
+TERM_BUFS = 5
+STAGED_BUFS = 4
 
 
 def tile_picked_yqrdqn_grad_p_kernel(
@@ -31,31 +38,30 @@ def tile_picked_yqrdqn_grad_p_kernel(
     nc = tc.nc
     with ExitStack() as ctx:
         keep = ctx.enter_context(tc.tile_pool(name="keep", bufs=1))
-        ring = ctx.enter_context(tc.tile_pool(name="ring", bufs=4))
-        work = ctx.enter_context(tc.tile_pool(name="work", bufs=2))
+        work = ctx.enter_context(tc.tile_pool(name="work", bufs=SCALED_BUFS))
         psum = ctx.enter_context(tc.psum_pool(name="psum", bufs=1))
 
-        offs_t = keep.tile([P, S // 16], U16, name="offs_t")
-        nxt_t = keep.tile([P, S // 16], U16, name="nxt_t")
-        pa_t = keep.tile([P, U // 16], U16, name="pa_t")
-        pb_t = keep.tile([P, U // 16], U16, name="pb_t")
+        offs_t = keep.tile([P, S // LIST_ROWS], U16, name="offs_t")
+        nxt_t = keep.tile([P, S // LIST_ROWS], U16, name="nxt_t")
+        pa_t = keep.tile([P, U // LIST_ROWS], U16, name="pa_t")
+        pb_t = keep.tile([P, U // LIST_ROWS], U16, name="pb_t")
         xw = keep.tile([P, T], I32, name="xw")
         ew = keep.tile([P, W], I32, name="ew")
         xs = keep.tile([P, T], U8, name="xs")
-        es = keep.tile([P, W], U8, name="es")
-        wq_raw = keep.tile([P, 4, V], F32, name="wq_raw")
-        wt_raw = keep.tile([P, 4, V], F32, name="wt_raw")
+        es = keep.tile([P, W], U8, name="es", tag="wt_codes", align_bytes=64)
+        wq_raw = keep.tile([P, PACK, V], F32, name="wq_raw")
+        wt_raw = keep.tile([P, PACK, V], F32, name="wt_raw")
         rows = keep.tile([P, P], F32, name="rows")
         ident = keep.tile([P, P], F32, name="ident")
-        y_neg = keep.tile([P, TB * V + SPARE], F32, name="y_neg")
-        h_all = keep.tile([P, TB * V + SPARE], F32, name="h_all")
+        y_neg = keep.tile([P, T_BLOCKS * V + SPARE], F32, name="y_neg")
+        h_all = keep.tile([P, T_BLOCKS * V + SPARE], F32, name="h_all")
 
         nc.gpsimd.memset(xs[:].bitcast(I32), 0)
         nc.gpsimd.memset(es[:].bitcast(I32), 0)
         nc.gpsimd.memset(rows[:], 0.0)
         make_identity(nc, ident[:])
-        nc.gpsimd.memset(y_neg[:, TB * V :], 0.0)
-        nc.gpsimd.memset(h_all[:, TB * V :], 0.0)
+        nc.gpsimd.memset(y_neg[:, T_BLOCKS * V :], 0.0)
+        nc.gpsimd.memset(h_all[:, T_BLOCKS * V :], 0.0)
 
         def load_scale_rows(tile, scales):
             for q in range(4):
@@ -68,103 +74,111 @@ def tile_picked_yqrdqn_grad_p_kernel(
         nc.sync.dma_start(out=xw[:], in_=x_words[0].rearrange("p n t -> p (n t)").bitcast(I32))
         nc.sync.dma_start(nxt_t[:], nxt)
         load_scale_rows(xs, x_scales)
-        nc.sync.dma_start(out=wq_raw[:], in_=wq.rearrange("(p j) v -> p j v", j=4))
-        nc.sync.dma_start(out=wt_raw[:], in_=wt.rearrange("(p j) v -> p j v", j=4))
+        nc.sync.dma_start(out=wq_raw[:], in_=wq.rearrange("(p j) v -> p j v", j=PACK))
+        nc.sync.dma_start(out=wt_raw[:], in_=wt.rearrange("(p j) v -> p j v", j=PACK))
         load_scale_rows(es, e_scales)
         nc.sync.dma_start(pa_t[:], pa)
         nc.sync.dma_start(out=ew[:], in_=e_words[0].rearrange("p n t -> p (n t)").bitcast(I32))
         nc.sync.dma_start(pb_t[:], pb)
-        nc.sync.dma_start(out=rows[24:28, :], in_=disc.rearrange("(b c) o -> b (c o)", c=P))
-        nc.sync.dma_start(out=rows[28:32, :], in_=rew.rearrange("(b c) o -> b (c o)", c=P))
-        for i, row in enumerate((tau, ku, kd)):
+        disc_row = 3 * R_BLOCKS
+        rew_row = disc_row + T_BLOCKS
+        nc.sync.dma_start(out=rows[disc_row:rew_row, :], in_=disc.rearrange("(b c) o -> b (c o)", c=P))
+        nc.sync.dma_start(out=rows[rew_row : rew_row + T_BLOCKS, :], in_=rew.rearrange("(b c) o -> b (c o)", c=P))
+        for i, per_pair in enumerate((tau, ku, kd)):
             nc.sync.dma_start(
-                out=rows[RB * i : RB * (i + 1), :],
-                in_=row[0:1, :].rearrange("o (j c) -> (o j) c", c=P),
+                out=rows[R_BLOCKS * i : R_BLOCKS * (i + 1), :],
+                in_=per_pair[0:1, :].rearrange("o (j c) -> (o j) c", c=P),
             )
 
-        def gather_words(words, index, name, pieces):
-            codes = keep.tile([P, S], U32, name=name + "_codes", align_bytes=64)
+        def gather_words(words, index, name, pieces, tag):
+            codes = keep.tile([P, S], U32, name=name, tag=tag, align_bytes=64)
             n = S // pieces
             for i in range(pieces):
                 nc.vector.tensor_copy(
                     codes[:, i * n : (i + 1) * n],
-                    words[:].bitcast(U32).indirect(index[:, i * n // 16 : (i + 1) * n // 16]),
+                    words[:].bitcast(U32).indirect(index[:, i * n // LIST_ROWS : (i + 1) * n // LIST_ROWS]),
                 )
             return codes
 
         def gather_scales(scales, index, name):
-            plane = keep.tile([P, S], U8, name=name + "_plane", align_bytes=64)
-            nc.vector.tensor_copy(plane[:], scales[:].indirect(index[:]))
-            return plane
+            picked = keep.tile([P, S], U8, name=name, align_bytes=64)
+            nc.vector.tensor_copy(picked[:], scales[:].indirect(index[:]))
+            return picked
 
         def quantize_weight(raw, name):
-            grouped = keep.tile([P, V * 4], BF16, name=name + "_grouped", align_bytes=64)
+            grouped = keep.tile([P, V * PACK], BF16, name=name + "_grouped", align_bytes=64)
             codes = keep.tile([P, V], U32, name=name + "_codes", align_bytes=64)
-            plane = keep.tile([P, V], U8, name=name + "_plane", align_bytes=64)
+            scales = keep.tile([P, V], U8, name=name + "_scales", align_bytes=64)
             nc.scalar.copy(
-                out=grouped[:].rearrange("p (c i j) -> p c j i", i=4, j=4),
+                out=grouped[:].rearrange("p (c i j) -> p c j i", i=4, j=PACK),
                 in_=raw[:].rearrange("p j (c i) -> p c j i", i=4),
             )
-            nc.vector.quantize_mx(out=codes[:].bitcast(FP8X4), scales=plane[:], in_=grouped[:])
-            return codes, plane
+            nc.vector.quantize_mx(out=codes[:].bitcast(FP8X4), scales=scales[:], in_=grouped[:])
+            return codes, scales
 
-        def product(picked, weight, b, name):
-            acc = psum.tile([P, 512], F32, name=name, tag="acc", bufs=3)
+        def product(acc, picked, weight_mx, b):
             cols = slice(b * P, (b + 1) * P)
             nc.tensor.matmul_mx(
-                out=acc[:, :V],
+                out=acc,
                 lhsT=picked[0][:, cols].bitcast(FP8X4),
                 lhsT_scale=picked[1][:, cols],
-                rhs=weight[0][:].bitcast(FP8X4),
-                rhs_scale=weight[1][:],
+                rhs=weight_mx[0][:].bitcast(FP8X4),
+                rhs_scale=weight_mx[1][:],
                 start=True,
                 stop=True,
             )
-            return acc[:, :V]
 
         def place(b):
-            return (TB - 1 - b) * V
+            return (T_BLOCKS - 1 - b) * V
 
-        x_picked = (gather_words(xw, offs_t, "x", 1), gather_scales(xs, offs_t, "x"))
+        x_picked = (gather_words(xw, offs_t, "x_codes", 1, "x_codes"), gather_scales(xs, offs_t, "x_picked_scales"))
         wq_mx = quantize_weight(wq_raw, "wq")
-        e_plane = gather_scales(es, nxt_t, "e")
+        e_picked_scales = gather_scales(es, nxt_t, "e_picked_scales")
         wt_mx = quantize_weight(wt_raw, "wt")
-        for b in range(TB):
-            acc = product(x_picked, wq_mx, b, "y_acc")
-            nc.scalar.activation(y_neg[:, place(b) : place(b) + V], acc, ACT.Copy, scale=-1.0)
+        for b in range(T_BLOCKS):
+            y_acc = psum.tile([P, V], F32, name="y_acc", tag="td", bufs=TD_BANKS)
+            product(y_acc[:], x_picked, wq_mx, b)
+            nc.scalar.activation(y_neg[:, place(b) : place(b) + V], y_acc[:], ACT.Copy, scale=-1.0)
 
-        e_picked = (gather_words(ew, nxt_t, "e", 2), e_plane)
+        e_picked = (gather_words(ew, nxt_t, "e_codes", 2, "wt_grouped"), e_picked_scales)
 
-        turned = psum.tile([P, 512], F32, name="turned")
-        nc.tensor.transpose(turned[:, :P], rows[:], ident[:])
-        per_t = keep.tile([P, 2 * TB], F32, name="per_t")
-        nc.scalar.copy(per_t[:], turned[:, 24:32])
-        weight = keep.tile([P, 2 * RB], F32, name="weight")
-        slope_dn = keep.tile([P, RB], F32, name="slope_dn")
-        k_pos = keep.tile([P, 2 * RB], F32, name="k_pos")
-        k_neg = keep.tile([P, 2 * RB], F32, name="k_neg")
-        nc.scalar.copy(weight[:, :RB], turned[:, :RB])
-        nc.scalar.activation(weight[:, RB:], turned[:, :RB], ACT.Copy, scale=1.0, bias=-1.0)
-        nc.scalar.activation(slope_dn[:], turned[:, :RB], ACT.Copy, scale=-1.0, bias=1.0)
-        nc.scalar.activation(k_pos[:], turned[:, RB : 3 * RB], ACT.Relu)
-        nc.scalar.activation(k_neg[:], turned[:, RB : 3 * RB], ACT.Relu, scale=-1.0)
+        per_t = keep.tile([P, 2 * T_BLOCKS], F32, name="per_t")
+        per_r = keep.tile([P, 3 * R_BLOCKS], F32, name="per_r")
+        for half, (columns, first) in enumerate(((per_t, disc_row), (per_r, 0))):
+            turned = psum.tile([P, P], F32, name="turned", tag="h_bank%d" % half)
+            nc.tensor.transpose(turned[:], rows[:], ident[:])
+            nc.scalar.copy(columns[:], turned[:, first : first + columns.shape[1]])
 
-        for b in range(TB):
-            acc = product(e_picked, wt_mx, b, "h_acc")
-            nc.scalar.activation(
-                h_all[:, place(b) : place(b) + V],
-                acc,
-                ACT.Identity,
-                scale=per_t[:, b : b + 1],
-                bias=per_t[:, TB + b : TB + b + 1],
-            )
+        weight = keep.tile([P, 2 * R_BLOCKS], F32, name="weight")
+        slope_dn = keep.tile([P, R_BLOCKS], F32, name="slope_dn")
+        k_pos = keep.tile([P, 2 * R_BLOCKS], F32, name="k_pos")
+        k_neg = keep.tile([P, 2 * R_BLOCKS], F32, name="k_neg")
+        nc.scalar.copy(weight[:, :R_BLOCKS], per_r[:, :R_BLOCKS])
+        nc.scalar.activation(weight[:, R_BLOCKS:], per_r[:, :R_BLOCKS], ACT.Copy, scale=1.0, bias=-1.0)
+        nc.scalar.activation(slope_dn[:], per_r[:, :R_BLOCKS], ACT.Copy, scale=-1.0, bias=1.0)
+        nc.scalar.activation(k_pos[:], per_r[:, R_BLOCKS:], ACT.Relu)
+        nc.scalar.activation(k_neg[:], per_r[:, R_BLOCKS:], ACT.Relu, scale=-1.0)
 
-        span = keep.tile([P, 2 * RB], F32, name="span")
-        shift = keep.tile([P, 2 * RB], F32, name="shift")
-        span_lo = keep.tile([P, 2 * RB], F32, name="span_lo")
-        span_hi = keep.tile([P, 2 * RB], F32, name="span_hi")
-        lo = keep.tile([P, 2 * RB], F32, name="lo")
-        hi = keep.tile([P, 2 * RB], F32, name="hi")
+        for half in range(2):
+            h_acc = psum.tile([P, 2, V], F32, name="h_acc", tag="h_bank%d" % half)
+            for i in range(2):
+                product(h_acc[:, i, :], e_picked, wt_mx, 2 * half + i)
+            for i in range(2):
+                b = 2 * half + i
+                nc.scalar.activation(
+                    h_all[:, place(b) : place(b) + V],
+                    h_acc[:, i, :],
+                    ACT.Identity,
+                    scale=per_t[:, b : b + 1],
+                    bias=per_t[:, T_BLOCKS + b : T_BLOCKS + b + 1],
+                )
+
+        span = keep.tile([P, 2 * R_BLOCKS], F32, name="span")
+        shift = keep.tile([P, 2 * R_BLOCKS], F32, name="shift")
+        span_lo = keep.tile([P, 2 * R_BLOCKS], F32, name="span_lo")
+        span_hi = keep.tile([P, 2 * R_BLOCKS], F32, name="span_hi")
+        lo = keep.tile([P, 2 * R_BLOCKS], F32, name="lo")
+        hi = keep.tile([P, 2 * R_BLOCKS], F32, name="hi")
         nc.gpsimd.tensor_tensor(span[:], weight[:], k_pos[:], ALU.mult)
         nc.gpsimd.tensor_tensor(shift[:], weight[:], k_neg[:], ALU.mult)
         nc.gpsimd.tensor_scalar(span_lo[:], span[:], 0.0, None, ALU.min)
@@ -174,60 +188,77 @@ def tile_picked_yqrdqn_grad_p_kernel(
 
         out_view = out.rearrange("(b p) r -> p b r", p=P)
 
-        def gather_values(table, index, b, r0, width, name):
-            got = ring.tile([P, width], F32, name=name)
+        def gather_values(got, table, index, b, r0, width):
             window = V if width < V else V + SPARE
             nc.vector.tensor_copy(
-                got[:], table[:, place(b) : place(b) + window].indirect(index[:, r0 // 16 : (r0 + width) // 16])
+                got,
+                table[:, place(b) : place(b) + window].indirect(index[:, r0 // LIST_ROWS : (r0 + width) // LIST_ROWS]),
             )
-            return got
 
         def turn(dst, src, start, stop):
             nc.tensor.matmul(dst, lhsT=src, rhs=ident[:], is_transpose=True, start=start, stop=stop)
 
-        def clip_terms(td, j, n):
+        def clamp_terms(td, j, clamp_engine, upper_tag):
+            n = td.shape[1]
             terms = []
-            clamp = nc.vector if j >= VECTOR_FROM else nc.gpsimd
             for side, slope in enumerate((weight[:, j : j + 1], slope_dn[:, j : j + 1])):
-                scaled = work.tile([P, n], F32, name="scaled%d" % side)
-                term = work.tile([P, n], F32, name="term%d" % side, bufs=3)
-                c = side * RB + j
-                nc.scalar.activation(scaled[:], td, ACT.Copy, scale=slope)
-                clamp.tensor_scalar(term[:], scaled[:], hi[:, c : c + 1], lo[:, c : c + 1], ALU.min, ALU.max)
+                if side == 0 and upper_tag is not None:
+                    scaled = keep.tile([P, n], F32, name="scaled", tag=upper_tag)
+                else:
+                    scaled = work.tile([P, n], F32, name="scaled%d" % side)
+                term = work.tile([P, n], F32, name="term%d" % side, bufs=TERM_BUFS)
+                c = side * R_BLOCKS + j
+                nc.scalar.activation(scaled[:], td[:], ACT.Copy, scale=slope)
+                clamp_engine.tensor_scalar(term[:], scaled[:], hi[:, c : c + 1], lo[:, c : c + 1], ALU.min, ALU.max)
                 terms.append(term)
             return terms
 
-        def finish(terms, bank, j, b0, nb):
-            res = psum.tile([P, nb, P], F32, name="res", tag=bank)
+        def store_block(terms, j, b0, b1, copy_out):
+            nb = b1 - b0
+            res = psum.tile([P, nb, P], F32, name="res", bufs=OUT_BANKS)
             for side in range(2):
-                for b in range(nb):
-                    turn(res[:, b, :], terms[side][:, b * P : (b + 1) * P], side == 0 and b == 0, side == 1 and b == nb - 1)
-            staged = work.tile([P, nb, P], F32, name="staged", bufs=4)
-            nc.scalar.copy(staged[:], res[:])
-            nc.sync.dma_start(out=out_view[:, b0 : b0 + nb, j * P : (j + 1) * P], in_=staged[:])
+                for i in range(nb):
+                    first = side == 0 and i == 0
+                    final = side == 1 and i == nb - 1
+                    turn(res[:, i, :], terms[side][:, i * P : (i + 1) * P], first, final)
+            staged = work.tile([P, nb, P], F32, name="staged", bufs=STAGED_BUFS)
+            copy_out(staged[:], res[:])
+            nc.sync.dma_start(out=out_view[:, b0:b1, j * P : (j + 1) * P], in_=staged[:])
 
-        pending = None
-        unit = 0
+        y_got = keep.tile([P, T_BLOCKS * WIDEST], F32, name="y_got", tag="ew")
+
+        def gather_and_turn(h_got, tds, r0, width, b0, b1):
+            for b in range(b0, b1):
+                gather_values(h_got[:, b * width : (b + 1) * width], h_all, pb_t, b, r0, width)
+                for i, td in enumerate(tds):
+                    dst = td[:, (b - b0) * P : (b - b0 + 1) * P]
+                    turn(dst, h_got[:, b * width + i * P : b * width + (i + 1) * P], True, False)
+                    turn(dst, y_got[:, b * WIDEST + i * P : b * WIDEST + (i + 1) * P], False, True)
+
+        pending = []
         r0 = 0
-        for width in CHUNKS:
-            blocks = width // P
-            nb = TB // 2 if r0 + width == U else TB
-            y_got = [gather_values(y_neg, pa_t, b, r0, width, "y_got") for b in range(TB)]
-            for b0 in range(0, TB, nb):
-                banks = ["bank%d" % ((unit + i) % BANKS) for i in range(blocks)]
-                unit = unit + blocks
-                tds = [psum.tile([P, nb * P], F32, name="td", tag=bank) for bank in banks]
-                for b in range(nb):
-                    h_got = gather_values(h_all, pb_t, b0 + b, r0, width, "h_got")
-                    for i in range(blocks):
-                        cols = slice(i * P, (i + 1) * P)
-                        turn(tds[i][:, b * P : (b + 1) * P], y_got[b0 + b][:, cols], True, False)
-                        turn(tds[i][:, b * P : (b + 1) * P], h_got[:, cols], False, True)
-                for i in range(blocks):
-                    j = r0 // P + i
-                    terms = clip_terms(tds[i][:], j, nb * P)
-                    if pending is not None:
-                        finish(*pending)
-                    pending = (terms, banks[i], j, b0, nb)
+        for chunk, width in enumerate(CHUNKS):
+            j0 = r0 // P
+            h_got = keep.tile([P, T_BLOCKS * width], F32, name="h_got", tag="h_got%d" % max(chunk, 1))
+            for b in range(T_BLOCKS):
+                gather_values(y_got[:, b * WIDEST : b * WIDEST + width], y_neg, pa_t, b, r0, width)
+            older = pending
+            pending = []
+            if r0 + width < U:
+                tds = [psum.tile([P, S], F32, name="td", bufs=TD_BANKS) for i in range(width // P)]
+                gather_and_turn(h_got, tds, r0, width, 0, T_BLOCKS)
+                for i, td in enumerate(tds):
+                    terms = clamp_terms(td, j0 + i, nc.gpsimd, "h_got%d" % (chunk + 2) if i == 0 else None)
+                    pending.append((terms, j0 + i, 0, T_BLOCKS, nc.scalar.copy))
+            else:
+                halves = ((0, T_BLOCKS // 2, nc.scalar.copy), (T_BLOCKS // 2, T_BLOCKS, nc.vector.tensor_copy))
+                tds = [psum.tile([P, S // 2], F32, name="td", tag="h_bank%d" % half) for half in range(2)]
+                for td, (b0, b1, copy_out) in zip(tds, halves):
+                    gather_and_turn(h_got, [td], r0, width, b0, b1)
+                for td, (b0, b1, copy_out) in zip(tds, halves):
+                    pending.append((clamp_terms(td, j0, nc.vector, None), j0, b0, b1, copy_out))
+            for item in older:
+                store_block(*item)
             r0 = r0 + width
-        finish(*pending)
+        for item in pending:
+            store_block(*item)

@@ -23,13 +23,17 @@ T_BLOCKS = S // P
 R_BLOCKS = U // P
 
 CHUNKS = (256, 256, 256, 128, 128)
-WIDEST = max(CHUNKS)
-SPARE = 96
+Y_FIRST = CHUNKS[0] + CHUNKS[1]
+VECTOR_HELPS_FROM = R_BLOCKS - 3
 TD_BANKS = 3
 OUT_BANKS = 3
 SCALED_BUFS = 3
 TERM_BUFS = 5
 STAGED_BUFS = 4
+
+
+def window_columns(width):
+    return V if width < V else width * 11 // 8
 
 
 def tile_picked_yqrdqn_grad_p_kernel(
@@ -53,8 +57,8 @@ def tile_picked_yqrdqn_grad_p_kernel(
         wt_raw = keep.tile([P, PACK, V], F32, name="wt_raw")
         rows = keep.tile([P, P], F32, name="rows")
         ident = keep.tile([P, P], F32, name="ident")
-        y_neg = keep.tile([P, T_BLOCKS * V + SPARE], F32, name="y_neg")
-        h_all = keep.tile([P, T_BLOCKS * V + SPARE], F32, name="h_all")
+        y_neg = keep.tile([P, (T_BLOCKS - 1) * V + window_columns(Y_FIRST)], F32, name="y_neg")
+        h_all = keep.tile([P, (T_BLOCKS - 1) * V + window_columns(max(CHUNKS))], F32, name="h_all")
 
         nc.gpsimd.memset(xs[:].bitcast(I32), 0)
         nc.gpsimd.memset(es[:].bitcast(I32), 0)
@@ -128,7 +132,7 @@ def tile_picked_yqrdqn_grad_p_kernel(
                 stop=True,
             )
 
-        def place(b):
+        def y_place(b):
             return (T_BLOCKS - 1 - b) * V
 
         x_picked = (gather_words(xw, offs_t, "x_codes", 1, "x_codes"), gather_scales(xs, offs_t, "x_picked_scales"))
@@ -138,7 +142,7 @@ def tile_picked_yqrdqn_grad_p_kernel(
         for b in range(T_BLOCKS):
             y_acc = psum.tile([P, V], F32, name="y_acc", tag="td", bufs=TD_BANKS)
             product(y_acc[:], x_picked, wq_mx, b)
-            nc.scalar.activation(y_neg[:, place(b) : place(b) + V], y_acc[:], ACT.Copy, scale=-1.0)
+            nc.scalar.activation(y_neg[:, y_place(b) : y_place(b) + V], y_acc[:], ACT.Copy, scale=-1.0)
 
         e_picked = (gather_words(ew, nxt_t, "e_codes", 2, "wt_grouped"), e_picked_scales)
 
@@ -166,7 +170,7 @@ def tile_picked_yqrdqn_grad_p_kernel(
             for i in range(2):
                 b = 2 * half + i
                 nc.scalar.activation(
-                    h_all[:, place(b) : place(b) + V],
+                    h_all[:, b * V : (b + 1) * V],
                     h_acc[:, i, :],
                     ACT.Identity,
                     scale=per_t[:, b : b + 1],
@@ -188,17 +192,19 @@ def tile_picked_yqrdqn_grad_p_kernel(
 
         out_view = out.rearrange("(b p) r -> p b r", p=P)
 
-        def gather_values(got, table, index, b, r0, width):
-            window = V if width < V else V + SPARE
-            nc.vector.tensor_copy(
-                got,
-                table[:, place(b) : place(b) + window].indirect(index[:, r0 // LIST_ROWS : (r0 + width) // LIST_ROWS]),
-            )
+        def gather_values(got, window, index, r0, width):
+            nc.vector.tensor_copy(got, window.indirect(index[:, r0 // LIST_ROWS : (r0 + width) // LIST_ROWS]))
+
+        def y_window(b, width):
+            return y_neg[:, y_place(b) : y_place(b) + window_columns(width)]
+
+        def h_window(b, width):
+            return h_all[:, b * V : (b + 1) * V] if width < V else h_all[:, b * V :]
 
         def turn(dst, src, start, stop):
             nc.tensor.matmul(dst, lhsT=src, rhs=ident[:], is_transpose=True, start=start, stop=stop)
 
-        def clamp_terms(td, j, clamp_engine, upper_tag):
+        def clamp_terms(td, j, clamp_engines, upper_tag):
             n = td.shape[1]
             terms = []
             for side, slope in enumerate((weight[:, j : j + 1], slope_dn[:, j : j + 1])):
@@ -209,7 +215,9 @@ def tile_picked_yqrdqn_grad_p_kernel(
                 term = work.tile([P, n], F32, name="term%d" % side, bufs=TERM_BUFS)
                 c = side * R_BLOCKS + j
                 nc.scalar.activation(scaled[:], td[:], ACT.Copy, scale=slope)
-                clamp_engine.tensor_scalar(term[:], scaled[:], hi[:, c : c + 1], lo[:, c : c + 1], ALU.min, ALU.max)
+                clamp_engines[side].tensor_scalar(
+                    term[:], scaled[:], hi[:, c : c + 1], lo[:, c : c + 1], ALU.min, ALU.max
+                )
                 terms.append(term)
             return terms
 
@@ -225,38 +233,48 @@ def tile_picked_yqrdqn_grad_p_kernel(
             copy_out(staged[:], res[:])
             nc.sync.dma_start(out=out_view[:, b0:b1, j * P : (j + 1) * P], in_=staged[:])
 
-        y_got = keep.tile([P, T_BLOCKS * WIDEST], F32, name="y_got", tag="ew")
+        y_early = keep.tile([P, Y_FIRST], F32, name="y_early")
+        y_late = keep.tile([P, (T_BLOCKS - 1) * Y_FIRST], F32, name="y_late", tag="ew")
+        y_slots = [y_early[:]] + [y_late[:, i * Y_FIRST : (i + 1) * Y_FIRST] for i in range(T_BLOCKS - 1)]
+        for b in range(T_BLOCKS):
+            gather_values(y_slots[b], y_window(b, Y_FIRST), pa_t, 0, Y_FIRST)
 
-        def gather_and_turn(h_got, tds, r0, width, b0, b1):
+        def gather_and_turn(h_got, y_got, tds, r0, width, b0, b1):
             for b in range(b0, b1):
-                gather_values(h_got[:, b * width : (b + 1) * width], h_all, pb_t, b, r0, width)
+                gather_values(h_got[:, b * width : (b + 1) * width], h_window(b, width), pb_t, r0, width)
                 for i, td in enumerate(tds):
                     dst = td[:, (b - b0) * P : (b - b0 + 1) * P]
                     turn(dst, h_got[:, b * width + i * P : b * width + (i + 1) * P], True, False)
-                    turn(dst, y_got[:, b * WIDEST + i * P : b * WIDEST + (i + 1) * P], False, True)
+                    turn(dst, y_got[b][:, i * P : (i + 1) * P], False, True)
 
         pending = []
         r0 = 0
         for chunk, width in enumerate(CHUNKS):
             j0 = r0 // P
-            h_got = keep.tile([P, T_BLOCKS * width], F32, name="h_got", tag="h_got%d" % max(chunk, 1))
-            for b in range(T_BLOCKS):
-                gather_values(y_got[:, b * WIDEST : b * WIDEST + width], y_neg, pa_t, b, r0, width)
+            h_got = keep.tile([P, T_BLOCKS * width], F32, name="h_got", tag="h_got%d" % chunk)
+            y0 = min(r0, CHUNKS[0])
+            y_got = [slot[:, y0 : y0 + width] for slot in y_slots]
+            if r0 >= Y_FIRST:
+                for b in range(T_BLOCKS):
+                    gather_values(y_got[b], y_window(b, width), pa_t, r0, width)
             older = pending
             pending = []
             if r0 + width < U:
                 tds = [psum.tile([P, S], F32, name="td", bufs=TD_BANKS) for i in range(width // P)]
-                gather_and_turn(h_got, tds, r0, width, 0, T_BLOCKS)
+                gather_and_turn(h_got, y_got, tds, r0, width, 0, T_BLOCKS)
                 for i, td in enumerate(tds):
-                    terms = clamp_terms(td, j0 + i, nc.gpsimd, "h_got%d" % (chunk + 2) if i == 0 else None)
-                    pending.append((terms, j0 + i, 0, T_BLOCKS, nc.scalar.copy))
+                    j = j0 + i
+                    engines = (nc.gpsimd, nc.vector if j >= VECTOR_HELPS_FROM else nc.gpsimd)
+                    terms = clamp_terms(td, j, engines, "h_got%d" % (chunk + 2) if i == 0 else None)
+                    copy_out = nc.vector.tensor_copy if j == VECTOR_HELPS_FROM else nc.scalar.copy
+                    pending.append((terms, j, 0, T_BLOCKS, copy_out))
             else:
                 halves = ((0, T_BLOCKS // 2, nc.scalar.copy), (T_BLOCKS // 2, T_BLOCKS, nc.vector.tensor_copy))
                 tds = [psum.tile([P, S // 2], F32, name="td", tag="h_bank%d" % half) for half in range(2)]
                 for td, (b0, b1, copy_out) in zip(tds, halves):
-                    gather_and_turn(h_got, [td], r0, width, b0, b1)
+                    gather_and_turn(h_got, y_got, [td], r0, width, b0, b1)
                 for td, (b0, b1, copy_out) in zip(tds, halves):
-                    pending.append((clamp_terms(td, j0, nc.vector, None), j0, b0, b1, copy_out))
+                    pending.append((clamp_terms(td, j0, (nc.vector, nc.vector), None), j0, b0, b1, copy_out))
             for item in older:
                 store_block(*item)
             r0 = r0 + width

from contextlib import ExitStack

import concourse.mybir as mybir
from concourse.masks import make_identity

K, T, S, V, W, U = 512, 1024, 512, 256, 2048, 1024
FLOPS = 2 * 2 * K * S * V

F32 = mybir.dt.float32
BF16 = mybir.dt.bfloat16
I32 = mybir.dt.int32
U32 = mybir.dt.uint32
U16 = mybir.dt.uint16
U8 = mybir.dt.uint8
FP8X4 = mybir.dt.float8_e4m3fn_x4
ALU = mybir.AluOpType
ACT = mybir.ActivationFunctionType

P = 128
PACK = 4
LIST_ROWS = 16
T_BLOCKS = S // P
R_BLOCKS = U // P

CHUNKS = (256, 256, 256, 128, 128)
Y_FIRST = CHUNKS[0] + CHUNKS[1]
VECTOR_HELPS_FROM = R_BLOCKS - 3
TD_BANKS = 3
OUT_BANKS = 3
SCALED_BUFS = 3
TERM_BUFS = 5
STAGED_BUFS = 4


def window_columns(width):
    return V if width < V else width * 11 // 8


def tile_picked_yqrdqn_grad_p_kernel(
    tc, x_words, x_scales, e_words, e_scales, wq, wt, disc, rew, tau, ku, kd, offs, nxt, pa, pb, out
):
    nc = tc.nc
    with ExitStack() as ctx:
        keep = ctx.enter_context(tc.tile_pool(name="keep", bufs=1))
        work = ctx.enter_context(tc.tile_pool(name="work", bufs=SCALED_BUFS))
        psum = ctx.enter_context(tc.psum_pool(name="psum", bufs=1))

        offs_t = keep.tile([P, S // LIST_ROWS], U16, name="offs_t")
        nxt_t = keep.tile([P, S // LIST_ROWS], U16, name="nxt_t")
        pa_t = keep.tile([P, U // LIST_ROWS], U16, name="pa_t")
        pb_t = keep.tile([P, U // LIST_ROWS], U16, name="pb_t")
        xw = keep.tile([P, T], I32, name="xw")
        ew = keep.tile([P, W], I32, name="ew")
        xs = keep.tile([P, T], U8, name="xs")
        es = keep.tile([P, W], U8, name="es", tag="wt_codes", align_bytes=64)
        wq_raw = keep.tile([P, PACK, V], F32, name="wq_raw")
        wt_raw = keep.tile([P, PACK, V], F32, name="wt_raw")
        rows = keep.tile([P, P], F32, name="rows")
        ident = keep.tile([P, P], F32, name="ident")
        y_neg = keep.tile([P, (T_BLOCKS - 1) * V + window_columns(Y_FIRST)], F32, name="y_neg")
        h_all = keep.tile([P, (T_BLOCKS - 1) * V + window_columns(max(CHUNKS))], F32, name="h_all")

        nc.gpsimd.memset(xs[:].bitcast(I32), 0)
        nc.gpsimd.memset(es[:].bitcast(I32), 0)
        nc.gpsimd.memset(rows[:], 0.0)
        make_identity(nc, ident[:])
        nc.gpsimd.memset(y_neg[:, T_BLOCKS * V :], 0.0)
        nc.gpsimd.memset(h_all[:, T_BLOCKS * V :], 0.0)

        def load_scale_rows(tile, scales):
            for q in range(4):
                nc.sync.dma_start(
                    out=tile[32 * q : 32 * q + 4, :].bitcast(I32),
                    in_=scales[0, 4 * q : 4 * q + 4, :].bitcast(I32),
                )

        nc.sync.dma_start(offs_t[:], offs)
        nc.sync.dma_start(out=xw[:], in_=x_words[0].rearrange("p n t -> p (n t)").bitcast(I32))
        nc.sync.dma_start(nxt_t[:], nxt)
        load_scale_rows(xs, x_scales)
        nc.sync.dma_start(out=wq_raw[:], in_=wq.rearrange("(p j) v -> p j v", j=PACK))
        nc.sync.dma_start(out=wt_raw[:], in_=wt.rearrange("(p j) v -> p j v", j=PACK))
        load_scale_rows(es, e_scales)
        nc.sync.dma_start(pa_t[:], pa)
        nc.sync.dma_start(out=ew[:], in_=e_words[0].rearrange("p n t -> p (n t)").bitcast(I32))
        nc.sync.dma_start(pb_t[:], pb)
        disc_row = 3 * R_BLOCKS
        rew_row = disc_row + T_BLOCKS
        nc.sync.dma_start(out=rows[disc_row:rew_row, :], in_=disc.rearrange("(b c) o -> b (c o)", c=P))
        nc.sync.dma_start(out=rows[rew_row : rew_row + T_BLOCKS, :], in_=rew.rearrange("(b c) o -> b (c o)", c=P))
        for i, per_pair in enumerate((tau, ku, kd)):
            nc.sync.dma_start(
                out=rows[R_BLOCKS * i : R_BLOCKS * (i + 1), :],
                in_=per_pair[0:1, :].rearrange("o (j c) -> (o j) c", c=P),
            )

        def gather_words(words, index, name, pieces, tag):
            codes = keep.tile([P, S], U32, name=name, tag=tag, align_bytes=64)
            n = S // pieces
            for i in range(pieces):
                nc.vector.tensor_copy(
                    codes[:, i * n : (i + 1) * n],
                    words[:].bitcast(U32).indirect(index[:, i * n // LIST_ROWS : (i + 1) * n // LIST_ROWS]),
                )
            return codes

        def gather_scales(scales, index, name):
            picked = keep.tile([P, S], U8, name=name, align_bytes=64)
            nc.vector.tensor_copy(picked[:], scales[:].indirect(index[:]))
            return picked

        def quantize_weight(raw, name):
            grouped = keep.tile([P, V * PACK], BF16, name=name + "_grouped", align_bytes=64)
            codes = keep.tile([P, V], U32, name=name + "_codes", align_bytes=64)
            scales = keep.tile([P, V], U8, name=name + "_scales", align_bytes=64)
            nc.scalar.copy(
                out=grouped[:].rearrange("p (c i j) -> p c j i", i=4, j=PACK),
                in_=raw[:].rearrange("p j (c i) -> p c j i", i=4),
            )
            nc.vector.quantize_mx(out=codes[:].bitcast(FP8X4), scales=scales[:], in_=grouped[:])
            return codes, scales

        def product(acc, picked, weight_mx, b):
            cols = slice(b * P, (b + 1) * P)
            nc.tensor.matmul_mx(
                out=acc,
                lhsT=picked[0][:, cols].bitcast(FP8X4),
                lhsT_scale=picked[1][:, cols],
                rhs=weight_mx[0][:].bitcast(FP8X4),
                rhs_scale=weight_mx[1][:],
                start=True,
                stop=True,
            )

        def y_place(b):
            return (T_BLOCKS - 1 - b) * V

        x_picked = (gather_words(xw, offs_t, "x_codes", 1, "x_codes"), gather_scales(xs, offs_t, "x_picked_scales"))
        wq_mx = quantize_weight(wq_raw, "wq")
        e_picked_scales = gather_scales(es, nxt_t, "e_picked_scales")
        wt_mx = quantize_weight(wt_raw, "wt")
        for b in range(T_BLOCKS):
            y_acc = psum.tile([P, V], F32, name="y_acc", tag="td", bufs=TD_BANKS)
            product(y_acc[:], x_picked, wq_mx, b)
            nc.scalar.activation(y_neg[:, y_place(b) : y_place(b) + V], y_acc[:], ACT.Copy, scale=-1.0)

        e_picked = (gather_words(ew, nxt_t, "e_codes", 2, "wt_grouped"), e_picked_scales)

        per_t = keep.tile([P, 2 * T_BLOCKS], F32, name="per_t")
        per_r = keep.tile([P, 3 * R_BLOCKS], F32, name="per_r")
        for half, (columns, first) in enumerate(((per_t, disc_row), (per_r, 0))):
            turned = psum.tile([P, P], F32, name="turned", tag="h_bank%d" % half)
            nc.tensor.transpose(turned[:], rows[:], ident[:])
            nc.scalar.copy(columns[:], turned[:, first : first + columns.shape[1]])

        weight = keep.tile([P, 2 * R_BLOCKS], F32, name="weight")
        slope_dn = keep.tile([P, R_BLOCKS], F32, name="slope_dn")
        k_pos = keep.tile([P, 2 * R_BLOCKS], F32, name="k_pos")
        k_neg = keep.tile([P, 2 * R_BLOCKS], F32, name="k_neg")
        nc.scalar.copy(weight[:, :R_BLOCKS], per_r[:, :R_BLOCKS])
        nc.scalar.activation(weight[:, R_BLOCKS:], per_r[:, :R_BLOCKS], ACT.Copy, scale=1.0, bias=-1.0)
        nc.scalar.activation(slope_dn[:], per_r[:, :R_BLOCKS], ACT.Copy, scale=-1.0, bias=1.0)
        nc.scalar.activation(k_pos[:], per_r[:, R_BLOCKS:], ACT.Relu)
        nc.scalar.activation(k_neg[:], per_r[:, R_BLOCKS:], ACT.Relu, scale=-1.0)

        for half in range(2):
            h_acc = psum.tile([P, 2, V], F32, name="h_acc", tag="h_bank%d" % half)
            for i in range(2):
                product(h_acc[:, i, :], e_picked, wt_mx, 2 * half + i)
            for i in range(2):
                b = 2 * half + i
                nc.scalar.activation(
                    h_all[:, b * V : (b + 1) * V],
                    h_acc[:, i, :],
                    ACT.Identity,
                    scale=per_t[:, b : b + 1],
                    bias=per_t[:, T_BLOCKS + b : T_BLOCKS + b + 1],
                )

        span = keep.tile([P, 2 * R_BLOCKS], F32, name="span")
        shift = keep.tile([P, 2 * R_BLOCKS], F32, name="shift")
        span_lo = keep.tile([P, 2 * R_BLOCKS], F32, name="span_lo")
        span_hi = keep.tile([P, 2 * R_BLOCKS], F32, name="span_hi")
        lo = keep.tile([P, 2 * R_BLOCKS], F32, name="lo")
        hi = keep.tile([P, 2 * R_BLOCKS], F32, name="hi")
        nc.gpsimd.tensor_tensor(span[:], weight[:], k_pos[:], ALU.mult)
        nc.gpsimd.tensor_tensor(shift[:], weight[:], k_neg[:], ALU.mult)
        nc.gpsimd.tensor_scalar(span_lo[:], span[:], 0.0, None, ALU.min)
        nc.gpsimd.tensor_scalar(span_hi[:], span[:], 0.0, None, ALU.max)
        nc.gpsimd.tensor_tensor(lo[:], span_lo[:], shift[:], ALU.subtract)
        nc.gpsimd.tensor_tensor(hi[:], span_hi[:], shift[:], ALU.subtract)

        out_view = out.rearrange("(b p) r -> p b r", p=P)

        def gather_values(got, window, index, r0, width):
            nc.vector.tensor_copy(got, window.indirect(index[:, r0 // LIST_ROWS : (r0 + width) // LIST_ROWS]))

        def y_window(b, width):
            return y_neg[:, y_place(b) : y_place(b) + window_columns(width)]

        def h_window(b, width):
            return h_all[:, b * V : (b + 1) * V] if width < V else h_all[:, b * V :]

        def turn(dst, src, start, stop):
            nc.tensor.matmul(dst, lhsT=src, rhs=ident[:], is_transpose=True, start=start, stop=stop)

        def clamp_terms(td, j, clamp_engines, upper_tag):
            n = td.shape[1]
            terms = []
            for side, slope in enumerate((weight[:, j : j + 1], slope_dn[:, j : j + 1])):
                if side == 0 and upper_tag is not None:
                    scaled = keep.tile([P, n], F32, name="scaled", tag=upper_tag)
                else:
                    scaled = work.tile([P, n], F32, name="scaled%d" % side)
                term = work.tile([P, n], F32, name="term%d" % side, bufs=TERM_BUFS)
                c = side * R_BLOCKS + j
                nc.scalar.activation(scaled[:], td[:], ACT.Copy, scale=slope)
                clamp_engines[side].tensor_scalar(
                    term[:], scaled[:], hi[:, c : c + 1], lo[:, c : c + 1], ALU.min, ALU.max
                )
                terms.append(term)
            return terms

        def store_block(terms, j, b0, b1, copy_out):
            nb = b1 - b0
            res = psum.tile([P, nb, P], F32, name="res", bufs=OUT_BANKS)
            for side in range(2):
                for i in range(nb):
                    first = side == 0 and i == 0
                    final = side == 1 and i == nb - 1
                    turn(res[:, i, :], terms[side][:, i * P : (i + 1) * P], first, final)
            staged = work.tile([P, nb, P], F32, name="staged", bufs=STAGED_BUFS)
            copy_out(staged[:], res[:])
            nc.sync.dma_start(out=out_view[:, b0:b1, j * P : (j + 1) * P], in_=staged[:])

        y_early = keep.tile([P, Y_FIRST], F32, name="y_early")
        y_late = keep.tile([P, (T_BLOCKS - 1) * Y_FIRST], F32, name="y_late", tag="ew")
        y_slots = [y_early[:]] + [y_late[:, i * Y_FIRST : (i + 1) * Y_FIRST] for i in range(T_BLOCKS - 1)]
        for b in range(T_BLOCKS):
            gather_values(y_slots[b], y_window(b, Y_FIRST), pa_t, 0, Y_FIRST)

        def gather_and_turn(h_got, y_got, tds, r0, width, b0, b1):
            for b in range(b0, b1):
                gather_values(h_got[:, b * width : (b + 1) * width], h_window(b, width), pb_t, r0, width)
                for i, td in enumerate(tds):
                    dst = td[:, (b - b0) * P : (b - b0 + 1) * P]
                    turn(dst, h_got[:, b * width + i * P : b * width + (i + 1) * P], True, False)
                    turn(dst, y_got[b][:, i * P : (i + 1) * P], False, True)

        pending = []
        r0 = 0
        for chunk, width in enumerate(CHUNKS):
            j0 = r0 // P
            h_got = keep.tile([P, T_BLOCKS * width], F32, name="h_got", tag="h_got%d" % chunk)
            y0 = min(r0, CHUNKS[0])
            y_got = [slot[:, y0 : y0 + width] for slot in y_slots]
            if r0 >= Y_FIRST:
                for b in range(T_BLOCKS):
                    gather_values(y_got[b], y_window(b, width), pa_t, r0, width)
            older = pending
            pending = []
            if r0 + width < U:
                tds = [psum.tile([P, S], F32, name="td", bufs=TD_BANKS) for i in range(width // P)]
                gather_and_turn(h_got, y_got, tds, r0, width, 0, T_BLOCKS)
                for i, td in enumerate(tds):
                    j = j0 + i
                    engines = (nc.gpsimd, nc.vector if j >= VECTOR_HELPS_FROM else nc.gpsimd)
                    terms = clamp_terms(td, j, engines, "h_got%d" % (chunk + 2) if i == 0 else None)
                    copy_out = nc.vector.tensor_copy if j == VECTOR_HELPS_FROM else nc.scalar.copy
                    pending.append((terms, j, 0, T_BLOCKS, copy_out))
            else:
                halves = ((0, T_BLOCKS // 2, nc.scalar.copy), (T_BLOCKS // 2, T_BLOCKS, nc.vector.tensor_copy))
                tds = [psum.tile([P, S // 2], F32, name="td", tag="h_bank%d" % half) for half in range(2)]
                for td, (b0, b1, copy_out) in zip(tds, halves):
                    gather_and_turn(h_got, y_got, [td], r0, width, b0, b1)
                for td, (b0, b1, copy_out) in zip(tds, halves):
                    pending.append((clamp_terms(td, j0, (nc.vector, nc.vector), None), j0, b0, b1, copy_out))
            for item in older:
                store_block(*item)
            r0 = r0 + width
        for item in pending:
            store_block(*item)
